import numpy as np, ml_dtypes
CORES = [24,25,26,27,28,29,30,31]
N = 8
import mx_ref
BF = ml_dtypes.bfloat16
def entries(a):
    return np.ascontiguousarray(a.T).reshape(-1)
def table(e):
    return np.ascontiguousarray(np.reshape(e, (-1, 16)).T).astype(np.int32)
def cols(t, e):
    v = np.concatenate([t.reshape(128, -1, 4), np.zeros((128, 1, 4), BF)], axis=1)
    return np.ascontiguousarray(v[:, e]).reshape(128, -1)
def tile(rs):
    return np.stack(rs, axis=2).reshape(128, -1).astype(BF)
def f(rng, *shape):
    return mx_ref.flush((rng.standard_normal(shape, dtype=np.float32) * np.exp2(rng.integers(-2, 3, shape[:-1] + (1,)))).astype(BF))
def wide(rng, *shape, cols=0):
    v = rng.standard_normal(shape, dtype=np.float32) * np.exp2(rng.integers(-12, 13, shape)).astype(np.float32)
    if cols: v *= np.repeat(np.exp2(rng.integers(-cols, cols + 1, shape[:-2] + (1, shape[-1] // 4))) * (rng.random(shape[:-2] + (1, shape[-1] // 4)) > 0.0625), 4, axis=-1).astype(np.float32)
    return mx_ref.flush(v.astype(BF))
T, E, EC, CAPP = 256, 4, 128, 48
def lists(rng, case=""):
    sn, so = np.full((N, N, CAPP), -1), np.full((N, E, EC), -1)
    lone = rng.integers(0, N)
    for d in range(N):
        a = rng.integers(0, E)
        n = rng.integers(CAPP // 4, CAPP + 1, N)
        if case == "full": n[:] = CAPP
        if case == "empty": n[(d + 1) % N] = 0
        if case == "empty" and d == lone: n[np.arange(N) != d] = 0
        used = np.concatenate([s * CAPP + (np.arange(n[s]) if case == "sorted" else rng.permutation(CAPP)[:n[s]]) for s in range(N)])
        if case == "one": used = rng.permutation(N * CAPP)[:EC + rng.integers(E - 1, 8 * E - 7)]
        if case != "sorted": used = rng.permutation(used)
        if case == "empty": used = used[:(E - 1) * EC]
        key = rng.random((E, EC)) * np.exp2(rng.integers(-1, 2, (E, 1)))
        if case in ("full", "one"): key[a] = -1
        if case == "empty": key[a] = 9
        who = np.argsort(key.reshape(-1))[:len(used)] // EC
        if case == "sorted": who = np.sort(who)
        for m in range(E):
            k = used[who == m]; so[d, m, :len(k)] = k
        sn[used // CAPP, d, used % CAPP] = rng.integers(0, T, len(used))
        if case == "sorted":
            for s in range(N): sn[s, d, :n[s]] = np.sort(sn[s, d, :n[s]])
    return {"sn": np.stack([table(q) for q in sn]), "so": np.stack([table(q) for q in so])}
def setup_inputs(rng):
    return {"x": f(rng, N, 128, 4 * T), "w": f(rng, N, 128, 2048 * E), "v": f(rng, N, 128, 512 * E), **lists(rng)}
def setup_inputs_full(rng):
    return {**setup_inputs(rng), **lists(rng, "full")}
def setup_inputs_one(rng):
    return {**setup_inputs(rng), **lists(rng, "one")}
def setup_inputs_empty(rng):
    return {**setup_inputs(rng), **lists(rng, "empty")}
def setup_inputs_sorted(rng):
    return {**setup_inputs(rng), **lists(rng, "sorted")}
def setup_inputs_spread(rng):
    d = setup_inputs(rng); d["x"] = wide(rng, N, 128, 4 * T, cols=6); return d
def check_inputs(d):
    b = []
    for r in range(N):
        c, e = entries(d["sn"][r]), entries(d["so"][r]).reshape(E, EC)
        if c.min() < -1 or c.max() >= T: b.append("sn")
        got = np.concatenate([entries(d["sn"][s])[r * CAPP:(r + 1) * CAPP] for s in range(N)])
        if e.min() < -1 or ((e[:, 1:] >= 0) & (e[:, :-1] < 0)).any() or np.sort(e[e >= 0]).tolist() != np.flatnonzero(got >= 0).tolist(): b.append("so")
    return b
def reference(x, w, v, sn, so):
    y = np.zeros((N, 128, E * EC), np.float32)
    for r in range(N):
        arrived = np.concatenate([cols(x[s], entries(sn[s])[r * CAPP:(r + 1) * CAPP]) for s in range(N)], axis=1)
        e = entries(so[r])
        for m in range(E):
            k = e[EC * m:EC * m + EC]
            t = mx_ref.quantize(cols(arrived, k))
            R = []
            for i in range(4):
                W = mx_ref.quantize(np.ascontiguousarray(w[r][:, 2048 * m + 512 * i:2048 * m + 512 * i + 512]))
                R.append(np.maximum(mx_ref.matmul(W, t), np.float32(0)) * np.float32(0.05))
            z = mx_ref.matmul(mx_ref.quantize(np.ascontiguousarray(v[r][:, 512 * m:512 * m + 512])), mx_ref.quantize(tile(R)))
            y[r][:, EC * m:EC * m + EC] = np.where(k >= 0, z, np.float32(0))
    return {"y": y}

@@ -1,0 +1,235 @@
+from concourse.bass import DstId, RemoteDMATransfer
+from concourse.mybir import dt, AluOpType, ActivationFunctionType
+
+E, EC, CAPP, NR, TOK = 4, 128, 48, 8, 256
+F8 = "float8_e4m3fn_x4"
+WIN = EC + NR * CAPP
+XP = {"0": (0, 128), "1": (128, 256)}
+WP = {"0": (0, 4), "1": (4, 8), "2": (8, 12), "3": (12, 14), "3b": (14, 16)}
+VP = {"a": (0, 2), "b": (2, 4)}
+SYNC = "Lx0 Lx1 Ln5 Ln6 Ln7 Lw0 ?xl1 Lva Lw1 ?wl0 Lw2 ?loc Lw3 Lw3b Lvb".split()
+ACT0 = "Ln0 Ln1 Ln2 Ln3 Ln4 Lo0 Lo1 Lo2 Lo3 Lo4 Lo5 Lo6 Lo7".split()
+VECTOR = "w0 ua w1 ?ready ?arrc p0 p1 ?arrs s1 p23 w2 e12 h0 e11 w3 h1 w3b e30 ub h2 e33 h3 y2 y3".split()
+TENSOR = "m02 m00 m03 m01 m12 m13 m10 m11 m21 m22 v0 m20 m30 v1 m23 m32 m31 m33 v2 v3".split()
+SCALAR = "?ready ?arrs s0 s23 e02 e00 e01 e03 e13 e10 e21 e22 y0 e20 y1 e23 e32 e31".split()
+STORES = (0, 1, 2, 3)
+SCRATCH = {
+    "snt": ("sbuf", [128, 24], "int32"),
+    "sot": ("sbuf", [128, 32], "int32"),
+    "offs": ("sbuf", [128, 32], "uint16"),
+    "offt": ("sbuf", [128, 32], "uint16"),
+    "xt": ("sbuf", [128, 4 * TOK], "bfloat16"),
+    "xq": ("sbuf", [128, TOK], F8),
+    "xs": ("sbuf", [128, TOK], "uint8"),
+    "slotq": ("sbuf", [128, (NR - 1) * CAPP], F8),
+    "slots": ("sbuf", [128, (NR - 1) * CAPP], "uint8"),
+    "zt": ("sbuf", [128, 4 * EC], "bfloat16"),
+    "landq": ("sbuf", [128, WIN], F8),
+    "lands": ("sbuf", [128, WIN], "uint8"),
+    "tokq": ("sbuf", [128, E * EC], F8),
+    "toks": ("sbuf", [128, E * EC], "uint8"),
+    "wt": ("sbuf", [128, 2048 * E], "bfloat16"),
+    "wq": ("sbuf", [128, 512 * E], F8),
+    "ws": ("sbuf", [128, 512 * E], "uint8"),
+    "vt": ("sbuf", [128, 512 * E], "bfloat16"),
+    "vq": ("sbuf", [128, 128 * E], F8),
+    "vs": ("sbuf", [128, 128 * E], "uint8"),
+    "ht": ("sbuf", [128, 4 * EC * E], "bfloat16"),
+    "hq": ("sbuf", [128, EC * E], F8),
+    "hs": ("sbuf", [128, EC * E], "uint8"),
+    "yt": ("sbuf", [128, EC * E], "float32"),
+}
+for _i in range(8):
+    SCRATCH["ps%d" % _i] = ("psum", [128, 512], "float32")
+PICKS = {_k + _d: _o for _o in VECTOR + SCALAR if _o[0] in "ps" for _k in _o[0] for _d in _o[1:]}
+SEMAPHORES = ["snl", "sol", "zm", "zq", "cv", "cvo", "cvt", "xqd", "pc", "psc", "oc", "osc", "arrc", "arrs", "loc", "yd"]
+SEMAPHORES += ["xl" + _t for _t in XP] + ["wl" + _t for _t in WP] + ["wqd" + _t for _t in WP] + ["vl" + _t for _t in VP] + ["vqd" + _t for _t in VP]
+SEMAPHORES += sorted({_o for _o in TENSOR + VECTOR + SCALAR if _o[0] in "psmehvy"})
+
+
+def rank_program(g, core, T, topo):
+    r = T.rank_of(core)
+    if r is None:
+        return
+    S, V, A, P = T.sem, g.vector, g.scalar, g.tensor
+    COPY, RELU = ActivationFunctionType.Copy, ActivationFunctionType.Relu
+    narr = 2 * (NR - 1)
+
+    def u32(ap):
+        return ap.bitcast(dt.uint32)
+
+    def bank(m, b):
+        return T["ps%d" % (4 * (m % 2) + b)][:, 0:EC]
+
+    def cols(m):
+        return slice(EC * m, EC * m + EC)
+
+    def piece(pieces, i):
+        return [t for t in pieces if pieces[t][0] <= i < pieces[t][1]][0]
+
+    def wait(q, s):
+        if s == "ready":
+            q.wait_ge(S.cvt, 1)
+            q.wait_ge(S.zq, 1)
+            q.wait_ge(S.oc if q is V else S.osc, 1)
+        elif s == "arrs" and q is V:
+            q.wait_ge(S.osc, 1)
+            q.wait_ge(S.arrs, narr)
+        elif s in ("arrc", "arrs"):
+            q.wait_ge(S[s], narr)
+        elif s == "loc":
+            q.wait_ge(S.loc, 2 * narr)
+        else:
+            q.wait_ge(S[s], 128 if s in ("snl", "sol") else 16)
+
+    def load(q, op):
+        k, t = op[0], op[1:]
+        if k == "x":
+            a, b = XP[t]
+            q.dma_start(T.xt[:, 4 * a:4 * b], T.x[:, 4 * a:4 * b]).then_inc(S["xl" + t], 16)
+        elif k in "no":
+            i = int(t)
+            dst, src = (T.snt, T.sn) if k == "n" else (T.sot, T.so)
+            q.dma_start(dst[16 * i:16 * i + 16, :], src[:, :]).then_inc(S.snl if k == "n" else S.sol, 16)
+        elif k == "w":
+            a, b = WP[t]
+            q.dma_start(T.wt[:, 512 * a:512 * b], T.w[:, 512 * a:512 * b]).then_inc(S["wl" + t], 16)
+        elif k == "v":
+            a, b = VP[t]
+            q.dma_start(T.vt[:, 512 * a:512 * b], T.v[:, 512 * a:512 * b]).then_inc(S["vl" + t], 16)
+
+    def work(q, op):
+        k, t = op[0], op[1:]
+        if k == "?":
+            return wait(q, t)
+        if k == "L":
+            return load(q, t)
+        if k in "wu":
+            n = "w" if k == "w" else "v"
+            a, b = (WP if k == "w" else VP)[t]
+            q.wait_ge(S[n + "l" + t], 16)
+            q.quantize_mx(T[n + "q"][:, 128 * a:128 * b], T[n + "s"][:, 128 * a:128 * b], T[n + "t"][:, 512 * a:512 * b]).then_inc(S[n + "qd" + t], 1)
+            return
+        m = int(op[1])
+        b = int(op[2]) if k in "me" else 0
+        done = S[op]
+        if k in "ps":
+            n = len(op) - 1
+            to, off = slice(EC * m, EC * (m + n)), T.offt[:, 8 * m:8 * (m + n)]
+            if k == "p":
+                q.tensor_copy(u32(T.tokq[:, to]), u32(T.landq[:, :]).indirect(off)).then_inc(done, 1)
+            elif q is A:
+                q.activation(T.toks[:, to], T.lands[:, :].indirect(off), COPY).then_inc(done, 1)
+            else:
+                q.tensor_copy(T.toks[:, to], T.lands[:, :].indirect(off)).then_inc(done, 1)
+        elif k == "m":
+            q.wait_ge(S[PICKS["p%d" % m]], 1)
+            q.wait_ge(S[PICKS["s%d" % m]], 1)
+            q.wait_ge(S["wqd" + piece(WP, 4 * m + b)], 1)
+            if m >= 2:
+                q.wait_ge(S["e%d%d" % (m - 2, b)], 1)
+                if b == 3:
+                    q.wait_ge(S["y%d" % (m - 2)], 1)
+            c = 512 * m + 128 * b
+            q.matmul_mx(bank(m, b), T.wq[:, c:c + 128], T.ws[:, c:c + 128], T.tokq[:, cols(m)], T.toks[:, cols(m)], True, True).then_inc(done, 1)
+        elif k == "e":
+            q.wait_ge(S["m" + op[1:]], 1)
+            h = T.ht[:, 512 * m + b:512 * m + 512:4]
+            if q is A:
+                q.activation(h, bank(m, b), RELU, scale=0.05).then_inc(done, 1)
+            else:
+                q.tensor_scalar(h, bank(m, b), 0.0, 0.05, AluOpType.max, AluOpType.mult).then_inc(done, 1)
+        elif k == "h":
+            for c in range(4):
+                q.wait_ge(S["e%d%d" % (m, c)], 1)
+            q.quantize_mx(T.hq[:, cols(m)], T.hs[:, cols(m)], T.ht[:, 512 * m:512 * m + 512]).then_inc(done, 1)
+        elif k == "v":
+            q.wait_ge(S["vqd" + piece(VP, m)], 1)
+            q.wait_ge(S["h%d" % m], 1)
+            q.matmul_mx(bank(m, 3), T.vq[:, cols(m)], T.vs[:, cols(m)], T.hq[:, cols(m)], T.hs[:, cols(m)], True, True).then_inc(done, 1)
+        elif k == "y":
+            q.wait_ge(S["v%d" % m], 1)
+            if q is A:
+                q.activation(T.yt[:, cols(m)], bank(m, 3), COPY).then_inc(done, 1)
+            else:
+                q.tensor_copy(T.yt[:, cols(m)], bank(m, 3)).then_inc(done, 1)
+
+    for op in SYNC:
+        work(g.sync, op)
+    for op in ACT0:
+        work(A, op)
+    V.memset(T.zt[:, :], 0.0).then_inc(S.zm, 1)
+    V.wait_ge(S.zm, 1)
+    V.quantize_mx(T.landq[:, 0:EC], T.lands[:, 0:EC], T.zt[:, :]).then_inc(S.zq, 1)
+    K = CAPP // 16
+    ncv = 0
+    V.wait_ge(S.snl, 128)
+    if r > 0:
+        V.tensor_copy(T.offs[:, 0:K * r], T.snt[:, 0:K * r]).then_inc(S.cv, 1)
+        ncv += 1
+    if r < NR - 1:
+        V.tensor_copy(T.offs[:, K * r:K * (NR - 1)], T.snt[:, K * (r + 1):K * NR]).then_inc(S.cv, 1)
+        ncv += 1
+    for t in XP:
+        a, b = XP[t]
+        V.wait_ge(S["xl" + t], 16)
+        V.quantize_mx(T.xq[:, a:b], T.xs[:, a:b], T.xt[:, 4 * a:4 * b]).then_inc(S.xqd, 1)
+    V.wait_ge(S.cv, ncv)
+    V.wait_ge(S.xqd, len(XP))
+    n7 = K * (NR - 1)
+    V.tensor_copy(u32(T.slotq[:, :]), u32(T.xq[:, :]).indirect(T.offs[:, 0:n7])).then_inc(S.pc, 1)
+    A.wait_ge(S.cv, ncv)
+    A.wait_ge(S.xqd, len(XP))
+    A.activation(T.slots[:, :], T.xs[:, :].indirect(T.offs[:, 0:n7]), COPY).then_inc(S.psc, 1)
+    o0 = n7 + n7 % 2
+    own = EC + CAPP * r
+    V.tensor_copy(T.offs[:, o0:o0 + K], T.snt[:, K * r:K * r + K]).then_inc(S.cvo, 1)
+    V.wait_ge(S.cvo, 1)
+    V.tensor_copy(u32(T.landq[:, own:own + CAPP]), u32(T.xq[:, :]).indirect(T.offs[:, o0:o0 + K])).then_inc(S.oc, 1)
+    A.wait_ge(S.cvo, 1)
+    A.activation(T.lands[:, own:own + CAPP], T.xs[:, :].indirect(T.offs[:, o0:o0 + K]), COPY).then_inc(S.osc, 1)
+    V.wait_ge(S.sol, 128)
+    V.tensor_scalar(T.offt[:, :], T.sot[:, :], EC, None, AluOpType.add).then_inc(S.cvt, 1)
+
+    far, near, plan = 0, 0, []
+    for i in range(1, NR):
+        d = (r + i) % NR
+        dst = T.cores[d]
+        e = topo.engines(core, dst)
+        if topo.die(dst) != topo.die(core):
+            use = e[0::2][2 * far:2 * far + 2]
+            far += 1
+        else:
+            use = e[1::2][2 * near:2 * near + 2]
+            near += 1
+        rid, pid, _ = topo.addr(dst)
+        plan.append((d if d < r else d - 1, DstId(rid=rid, pnc=pid), sum(1 << k for k in use)))
+
+    def send(codes):
+        ts = []
+        for j, did, mask in plan:
+            if codes:
+                src = T.slotq[:, CAPP * j:CAPP * j + CAPP].bitcast(dt.uint8)
+                dst = T.landq[:, own:own + CAPP].bitcast(dt.uint8)
+            else:
+                src = T.slots[:, CAPP * j:CAPP * j + CAPP]
+                dst = T.lands[:, own:own + CAPP]
+            ts.append(RemoteDMATransfer(dst_ids=[did], dma_engine_mask=mask, remote_sem=S.arrc if codes else S.arrs, src=src, dst=dst))
+        g.remote_dma_fused(ts, local_sem=S.loc)
+
+    g.wait_ge(S.pc, 1)
+    send(True)
+    g.wait_ge(S.psc, 1)
+    send(False)
+    g.wait_ge(S.loc, 2 * narr)
+
+    for op in TENSOR:
+        work(P, op)
+    for op in SCALAR:
+        work(A, op)
+    for op in VECTOR:
+        work(V, op)
+    for m in STORES:
+        g.sync.wait_ge(S["y%d" % m], 1)
+        g.sync.dma_start(T.y[:, cols(m)], T.yt[:, cols(m)]).then_inc(S.yd, 16)
+    g.sync.wait_ge(S.yd, 16 * E)

@@ -4,25 +4,31 @@ from concourse.mybir import dt, AluOpType, ActivationFunctionType
 E, EC, CAPP, NR, TOK = 4, 128, 48, 8, 256
 F8 = "float8_e4m3fn_x4"
 WIN = EC + NR * CAPP
+K = CAPP // 16
+N7 = K * (NR - 1)
 XP = {"0": (0, 128), "1": (128, 256)}
-WP = {"0": (0, 4), "1": (4, 8), "2": (8, 12), "3": (12, 14), "3b": (14, 16)}
-VP = {"a": (0, 2), "b": (2, 4)}
-SYNC = "Lx0 Lx1 Ln5 Ln6 Ln7 Lw0 ?xl1 Lva Lw1 ?wl0 Lw2 ?loc Lw3 Lw3b Lvb".split()
-ACT0 = "Ln0 Ln1 Ln2 Ln3 Ln4 Lo0 Lo1 Lo2 Lo3 Lo4 Lo5 Lo6 Lo7".split()
-VECTOR = "w0 ua w1 ?ready ?arrc p0 p1 ?arrs s1 p23 w2 e12 h0 e11 w3 h1 w3b e30 ub h2 e33 h3 y2 y3".split()
-TENSOR = "m02 m00 m03 m01 m12 m13 m10 m11 m21 m22 v0 m20 m30 v1 m23 m32 m31 m33 v2 v3".split()
-SCALAR = "?ready ?arrs s0 s23 e02 e00 e01 e03 e13 e10 e21 e22 y0 e20 y1 e23 e32 e31".split()
-STORES = (0, 1, 2, 3)
+WP = {"0": (0, 4), "1": (4, 8), "2": (8, 10), "2b": (10, 12), "3": (12, 14), "3b": (14, 16)}
+VP = {"0": (0, 1), "1": (1, 2), "2": (2, 3), "3": (3, 4)}
+SP = {"0": (0, 12), "1": (12, 24)}
+NE = {"c": 2, "s": 2}
+LP = 32
+SYNC = "Ln0 Lx0 Lx1 Lw0 ?xl1 Lw1 Lw2 ?locs Lw2b Lw3 Lw3b Lv0 Lv1 Lv2 Lv3 Y0 Y1 Y2 Y3".split()
+POOL = "Rs Rc ?locs ?locc".split()
+VECTOR = ("Z C x0 x1 S1 P0 P1 Co D O w0 w1 w2 "
+          "p0 p1 p23 w2b e03 w3 e12 w3b h0 e21 u0 u1 h1 e30 u2 h2 e33 u3 h3 y3").split()
+TENSOR = "m00 m01 m02 m03 m10 m11 m12 m13 m20 m21 m22 m23 m30 m31 m32 m33 v0 v1 v2 v3".split()
+SCALAR = ("Ln1 Lo0 Lo1 S0 Q "
+          "s0 s1 s23 e00 e01 e02 e10 e11 e13 e20 e22 e23 e31 e32 y0 y1 y2").split()
 SCRATCH = {
-    "snt": ("sbuf", [128, 24], "int32"),
-    "sot": ("sbuf", [128, 32], "int32"),
+    "snt": ("sbuf", [LP, 24], "int32"),
+    "sot": ("sbuf", [LP, 32], "int32"),
     "offs": ("sbuf", [128, 32], "uint16"),
     "offt": ("sbuf", [128, 32], "uint16"),
     "xt": ("sbuf", [128, 4 * TOK], "bfloat16"),
     "xq": ("sbuf", [128, TOK], F8),
     "xs": ("sbuf", [128, TOK], "uint8"),
-    "slotq": ("sbuf", [128, (NR - 1) * CAPP], F8),
-    "slots": ("sbuf", [128, (NR - 1) * CAPP], "uint8"),
+    "slotq": ("sbuf", [128, NR * CAPP], F8),
+    "slots": ("sbuf", [128, NR * CAPP], "uint8"),
     "zt": ("sbuf", [128, 4 * EC], "bfloat16"),
     "landq": ("sbuf", [128, WIN], F8),
     "lands": ("sbuf", [128, WIN], "uint8"),
@@ -42,9 +48,9 @@ SCRATCH = {
 for _i in range(8):
     SCRATCH["ps%d" % _i] = ("psum", [128, 512], "float32")
 PICKS = {_k + _d: _o for _o in VECTOR + SCALAR if _o[0] in "ps" for _k in _o[0] for _d in _o[1:]}
-SEMAPHORES = ["snl", "sol", "zm", "zq", "cv", "cvo", "cvt", "xqd", "pc", "psc", "oc", "osc", "arrc", "arrs", "loc", "yd"]
-SEMAPHORES += ["xl" + _t for _t in XP] + ["wl" + _t for _t in WP] + ["wqd" + _t for _t in WP] + ["vl" + _t for _t in VP] + ["vqd" + _t for _t in VP]
-SEMAPHORES += sorted({_o for _o in TENSOR + VECTOR + SCALAR if _o[0] in "psmehvy"})
+SEMAPHORES = ["snl", "sol", "zm", "arrc", "arrs", "locc", "locs", "yd"]
+SEMAPHORES += ["xl" + _t for _t in XP] + ["wl" + _t for _t in WP] + ["vl" + _t for _t in VP]
+SEMAPHORES += sorted({_o for _o in TENSOR + VECTOR + SCALAR if _o[0] in "ZCDxwuPSOQpsmehvy"})
 
 
 def rank_program(g, core, T, topo):
@@ -54,142 +60,27 @@ def rank_program(g, core, T, topo):
     S, V, A, P = T.sem, g.vector, g.scalar, g.tensor
     COPY, RELU = ActivationFunctionType.Copy, ActivationFunctionType.Relu
     narr = 2 * (NR - 1)
+    o0 = K * NR
+    own = EC + CAPP * r
+    full = {"snl": LP, "sol": LP, "C": 128 // LP, "D": 128 // LP, }
+    for k in NE:
+        full["arr" + k] = full["loc" + k] = NE[k] * (NR - 1)
 
     def u32(ap):
         return ap.bitcast(dt.uint32)
 
-    def bank(m, b):
-        return T["ps%d" % (4 * (m % 2) + b)][:, 0:EC]
+    def bank(op):
+        return T["ps%d" % (TENSOR.index(op) % 8)][:, 0:EC]
 
-    def cols(m):
-        return slice(EC * m, EC * m + EC)
+    def freed(op):
+        i = TENSOR.index(op) - 8
+        return [{"m": "e", "v": "y"}[TENSOR[i][0]] + TENSOR[i][1:]] if i >= 0 else []
+
+    def cols(m, n=1):
+        return slice(EC * m, EC * (m + n))
 
     def piece(pieces, i):
         return [t for t in pieces if pieces[t][0] <= i < pieces[t][1]][0]
-
-    def wait(q, s):
-        if s == "ready":
-            q.wait_ge(S.cvt, 1)
-            q.wait_ge(S.zq, 1)
-            q.wait_ge(S.oc if q is V else S.osc, 1)
-        elif s == "arrs" and q is V:
-            q.wait_ge(S.osc, 1)
-            q.wait_ge(S.arrs, narr)
-        elif s in ("arrc", "arrs"):
-            q.wait_ge(S[s], narr)
-        elif s == "loc":
-            q.wait_ge(S.loc, 2 * narr)
-        else:
-            q.wait_ge(S[s], 128 if s in ("snl", "sol") else 16)
-
-    def load(q, op):
-        k, t = op[0], op[1:]
-        if k == "x":
-            a, b = XP[t]
-            q.dma_start(T.xt[:, 4 * a:4 * b], T.x[:, 4 * a:4 * b]).then_inc(S["xl" + t], 16)
-        elif k in "no":
-            i = int(t)
-            dst, src = (T.snt, T.sn) if k == "n" else (T.sot, T.so)
-            q.dma_start(dst[16 * i:16 * i + 16, :], src[:, :]).then_inc(S.snl if k == "n" else S.sol, 16)
-        elif k == "w":
-            a, b = WP[t]
-            q.dma_start(T.wt[:, 512 * a:512 * b], T.w[:, 512 * a:512 * b]).then_inc(S["wl" + t], 16)
-        elif k == "v":
-            a, b = VP[t]
-            q.dma_start(T.vt[:, 512 * a:512 * b], T.v[:, 512 * a:512 * b]).then_inc(S["vl" + t], 16)
-
-    def work(q, op):
-        k, t = op[0], op[1:]
-        if k == "?":
-            return wait(q, t)
-        if k == "L":
-            return load(q, t)
-        if k in "wu":
-            n = "w" if k == "w" else "v"
-            a, b = (WP if k == "w" else VP)[t]
-            q.wait_ge(S[n + "l" + t], 16)
-            q.quantize_mx(T[n + "q"][:, 128 * a:128 * b], T[n + "s"][:, 128 * a:128 * b], T[n + "t"][:, 512 * a:512 * b]).then_inc(S[n + "qd" + t], 1)
-            return
-        m = int(op[1])
-        b = int(op[2]) if k in "me" else 0
-        done = S[op]
-        if k in "ps":
-            n = len(op) - 1
-            to, off = slice(EC * m, EC * (m + n)), T.offt[:, 8 * m:8 * (m + n)]
-            if k == "p":
-                q.tensor_copy(u32(T.tokq[:, to]), u32(T.landq[:, :]).indirect(off)).then_inc(done, 1)
-            elif q is A:
-                q.activation(T.toks[:, to], T.lands[:, :].indirect(off), COPY).then_inc(done, 1)
-            else:
-                q.tensor_copy(T.toks[:, to], T.lands[:, :].indirect(off)).then_inc(done, 1)
-        elif k == "m":
-            q.wait_ge(S[PICKS["p%d" % m]], 1)
-            q.wait_ge(S[PICKS["s%d" % m]], 1)
-            q.wait_ge(S["wqd" + piece(WP, 4 * m + b)], 1)
-            if m >= 2:
-                q.wait_ge(S["e%d%d" % (m - 2, b)], 1)
-                if b == 3:
-                    q.wait_ge(S["y%d" % (m - 2)], 1)
-            c = 512 * m + 128 * b
-            q.matmul_mx(bank(m, b), T.wq[:, c:c + 128], T.ws[:, c:c + 128], T.tokq[:, cols(m)], T.toks[:, cols(m)], True, True).then_inc(done, 1)
-        elif k == "e":
-            q.wait_ge(S["m" + op[1:]], 1)
-            h = T.ht[:, 512 * m + b:512 * m + 512:4]
-            if q is A:
-                q.activation(h, bank(m, b), RELU, scale=0.05).then_inc(done, 1)
-            else:
-                q.tensor_scalar(h, bank(m, b), 0.0, 0.05, AluOpType.max, AluOpType.mult).then_inc(done, 1)
-        elif k == "h":
-            for c in range(4):
-                q.wait_ge(S["e%d%d" % (m, c)], 1)
-            q.quantize_mx(T.hq[:, cols(m)], T.hs[:, cols(m)], T.ht[:, 512 * m:512 * m + 512]).then_inc(done, 1)
-        elif k == "v":
-            q.wait_ge(S["vqd" + piece(VP, m)], 1)
-            q.wait_ge(S["h%d" % m], 1)
-            q.matmul_mx(bank(m, 3), T.vq[:, cols(m)], T.vs[:, cols(m)], T.hq[:, cols(m)], T.hs[:, cols(m)], True, True).then_inc(done, 1)
-        elif k == "y":
-            q.wait_ge(S["v%d" % m], 1)
-            if q is A:
-                q.activation(T.yt[:, cols(m)], bank(m, 3), COPY).then_inc(done, 1)
-            else:
-                q.tensor_copy(T.yt[:, cols(m)], bank(m, 3)).then_inc(done, 1)
-
-    for op in SYNC:
-        work(g.sync, op)
-    for op in ACT0:
-        work(A, op)
-    V.memset(T.zt[:, :], 0.0).then_inc(S.zm, 1)
-    V.wait_ge(S.zm, 1)
-    V.quantize_mx(T.landq[:, 0:EC], T.lands[:, 0:EC], T.zt[:, :]).then_inc(S.zq, 1)
-    K = CAPP // 16
-    ncv = 0
-    V.wait_ge(S.snl, 128)
-    if r > 0:
-        V.tensor_copy(T.offs[:, 0:K * r], T.snt[:, 0:K * r]).then_inc(S.cv, 1)
-        ncv += 1
-    if r < NR - 1:
-        V.tensor_copy(T.offs[:, K * r:K * (NR - 1)], T.snt[:, K * (r + 1):K * NR]).then_inc(S.cv, 1)
-        ncv += 1
-    for t in XP:
-        a, b = XP[t]
-        V.wait_ge(S["xl" + t], 16)
-        V.quantize_mx(T.xq[:, a:b], T.xs[:, a:b], T.xt[:, 4 * a:4 * b]).then_inc(S.xqd, 1)
-    V.wait_ge(S.cv, ncv)
-    V.wait_ge(S.xqd, len(XP))
-    n7 = K * (NR - 1)
-    V.tensor_copy(u32(T.slotq[:, :]), u32(T.xq[:, :]).indirect(T.offs[:, 0:n7])).then_inc(S.pc, 1)
-    A.wait_ge(S.cv, ncv)
-    A.wait_ge(S.xqd, len(XP))
-    A.activation(T.slots[:, :], T.xs[:, :].indirect(T.offs[:, 0:n7]), COPY).then_inc(S.psc, 1)
-    o0 = n7 + n7 % 2
-    own = EC + CAPP * r
-    V.tensor_copy(T.offs[:, o0:o0 + K], T.snt[:, K * r:K * r + K]).then_inc(S.cvo, 1)
-    V.wait_ge(S.cvo, 1)
-    V.tensor_copy(u32(T.landq[:, own:own + CAPP]), u32(T.xq[:, :]).indirect(T.offs[:, o0:o0 + K])).then_inc(S.oc, 1)
-    A.wait_ge(S.cvo, 1)
-    A.activation(T.lands[:, own:own + CAPP], T.xs[:, :].indirect(T.offs[:, o0:o0 + K]), COPY).then_inc(S.osc, 1)
-    V.wait_ge(S.sol, 128)
-    V.tensor_scalar(T.offt[:, :], T.sot[:, :], EC, None, AluOpType.add).then_inc(S.cvt, 1)
 
     far, near, plan = 0, 0, []
     for i in range(1, NR):
@@ -203,11 +94,12 @@ def rank_program(g, core, T, topo):
             use = e[1::2][2 * near:2 * near + 2]
             near += 1
         rid, pid, _ = topo.addr(dst)
-        plan.append((d if d < r else d - 1, DstId(rid=rid, pnc=pid), sum(1 << k for k in use)))
+        plan.append((d, DstId(rid=rid, pnc=pid), use))
 
     def send(codes):
         ts = []
-        for j, did, mask in plan:
+        for j, did, use in plan:
+            mask = sum(1 << k for k in use[:NE["c" if codes else "s"]])
             if codes:
                 src = T.slotq[:, CAPP * j:CAPP * j + CAPP].bitcast(dt.uint8)
                 dst = T.landq[:, own:own + CAPP].bitcast(dt.uint8)
@@ -215,21 +107,123 @@ def rank_program(g, core, T, topo):
                 src = T.slots[:, CAPP * j:CAPP * j + CAPP]
                 dst = T.lands[:, own:own + CAPP]
             ts.append(RemoteDMATransfer(dst_ids=[did], dma_engine_mask=mask, remote_sem=S.arrc if codes else S.arrs, src=src, dst=dst))
-        g.remote_dma_fused(ts, local_sem=S.loc)
+        g.remote_dma_fused(ts, local_sem=S.locc if codes else S.locs)
 
-    g.wait_ge(S.pc, 1)
-    send(True)
-    g.wait_ge(S.psc, 1)
-    send(False)
-    g.wait_ge(S.loc, 2 * narr)
+    def load(q, op):
+        k, t = op[0], op[1:]
+        if k == "x":
+            a, b = XP[t]
+            q.dma_start(T.xt[:, 4 * a:4 * b], T.x[:, 4 * a:4 * b]).then_inc(S["xl" + t], 16)
+        elif k in "no":
+            i = int(t)
+            dst, src = (T.snt, T.sn) if k == "n" else (T.sot, T.so)
+            q.dma_start(dst[16 * i:16 * i + 16, :], src[:, :]).then_inc(S.snl if k == "n" else S.sol, 16)
+        else:
+            a, b = (WP if k == "w" else VP)[t]
+            q.dma_start(T[k + "t"][:, 512 * a:512 * b], T[k][:, 512 * a:512 * b]).then_inc(S[k + "l" + t], 16)
 
-    for op in TENSOR:
-        work(P, op)
-    for op in SCALAR:
-        work(A, op)
-    for op in VECTOR:
-        work(V, op)
-    for m in STORES:
-        g.sync.wait_ge(S["y%d" % m], 1)
-        g.sync.dma_start(T.y[:, cols(m)], T.yt[:, cols(m)]).then_inc(S.yd, 16)
-    g.sync.wait_ge(S.yd, 16 * E)
+    def pick(q, codes, to, win, off, done):
+        if codes:
+            q.tensor_copy(u32(to), u32(win).indirect(off)).then_inc(done, 1)
+        elif q is A:
+            q.activation(to, win.indirect(off), COPY).then_inc(done, 1)
+        else:
+            q.tensor_copy(to, win.indirect(off)).then_inc(done, 1)
+
+    def run(q, ops):
+        seen = set()
+
+        def need(*names):
+            for s in names:
+                if s not in seen:
+                    seen.add(s)
+                    q.wait_ge(S[s], full.get(s, 16 if s[1:2] == "l" else 1))
+
+        for op in ops:
+            k, t = op[0], op[1:]
+            if k == "?":
+                need(t)
+            elif k == "L":
+                load(q, t)
+            elif k == "R":
+                need(*[("P" if t == "c" else "S") + u for u in SP])
+                send(t == "c")
+            elif k == "Y":
+                need(*["y" + u for u in t])
+                c = cols(int(t[0]), len(t))
+                q.dma_start(T.y[:, c], T.yt[:, c]).then_inc(S.yd, 16)
+            elif k == "Z":
+                q.memset(T.zt[:, :], 0.0).then_inc(S.zm, 1)
+                need("zm")
+                q.quantize_mx(T.landq[:, 0:EC], T.lands[:, 0:EC], T.zt[:, :]).then_inc(S.Z, 1)
+            elif k == "C":
+                if t:
+                    need("C")
+                    q.tensor_copy(T.offs[:, o0:o0 + K], T.offs[:, K * r:K * r + K]).then_inc(S[op], 1)
+                else:
+                    need("snl")
+                    for p in range(0, 128, LP):
+                        q.tensor_copy(T.offs[p:p + LP, 0:o0], T.snt[:, :]).then_inc(S[op], 1)
+            elif k == "D":
+                need("sol")
+                for p in range(0, 128, LP):
+                    q.tensor_scalar(T.offt[p:p + LP, :], T.sot[:, :], EC, None, AluOpType.add).then_inc(S.D, 1)
+            elif k == "x":
+                a, b = XP[t]
+                need("xl" + t)
+                q.quantize_mx(T.xq[:, a:b], T.xs[:, a:b], T.xt[:, 4 * a:4 * b]).then_inc(S[op], 1)
+            elif k in "wu":
+                n = "w" if k == "w" else "v"
+                a, b = (WP if k == "w" else VP)[t]
+                need(n + "l" + t)
+                q.quantize_mx(T[n + "q"][:, 128 * a:128 * b], T[n + "s"][:, 128 * a:128 * b], T[n + "t"][:, 512 * a:512 * b]).then_inc(S[op], 1)
+            elif k in "PSOQ":
+                need("C" if k in "PS" else "Co", *["x" + u for u in XP])
+                codes = k in "PO"
+                if k in "PS":
+                    a, b = SP[t]
+                    to = (T.slotq if codes else T.slots)[:, 16 * a:16 * b]
+                else:
+                    a, b = o0, o0 + K
+                    to = (T.landq if codes else T.lands)[:, own:own + CAPP]
+                pick(q, codes, to, (T.xq if codes else T.xs)[:, :], T.offs[:, a:b], S[op])
+            elif k in "ps":
+                m, n, codes = int(t[0]), len(t), k == "p"
+                need("D", "Z", *(("O", "arrc") if codes else ("Q", "arrs")))
+                pick(q, codes, (T.tokq if codes else T.toks)[:, cols(m, n)], (T.landq if codes else T.lands)[:, :],
+                     T.offt[:, 8 * m:8 * (m + n)], S[op])
+            elif k == "m":
+                m, b = int(t[0]), int(t[1])
+                need(PICKS["s%d" % m], "w" + piece(WP, 4 * m + b), PICKS["p%d" % m], *freed(op))
+                c = 512 * m + 128 * b
+                q.matmul_mx(bank(op), T.wq[:, c:c + 128], T.ws[:, c:c + 128], T.tokq[:, cols(m)], T.toks[:, cols(m)], True, True).then_inc(S[op], 1)
+            elif k == "e":
+                m, b = int(t[0]), int(t[1])
+                need("m" + t)
+                h = T.ht[:, 512 * m + b:512 * m + 512:4]
+                if q is A:
+                    q.activation(h, bank("m" + t), RELU, scale=0.05).then_inc(S[op], 1)
+                else:
+                    q.tensor_scalar(h, bank("m" + t), 0.0, 0.05, AluOpType.max, AluOpType.mult).then_inc(S[op], 1)
+            elif k == "h":
+                m = int(t)
+                need(*["e%d%d" % (m, c) for c in range(4)])
+                q.quantize_mx(T.hq[:, cols(m)], T.hs[:, cols(m)], T.ht[:, 512 * m:512 * m + 512]).then_inc(S[op], 1)
+            elif k == "v":
+                m = int(t)
+                need("u" + piece(VP, m), "h" + t, *freed(op))
+                q.matmul_mx(bank(op), T.vq[:, cols(m)], T.vs[:, cols(m)], T.hq[:, cols(m)], T.hs[:, cols(m)], True, True).then_inc(S[op], 1)
+            elif k == "y":
+                m = int(t)
+                need("v" + t)
+                if q is A:
+                    q.activation(T.yt[:, cols(m)], bank("v" + t), COPY).then_inc(S[op], 1)
+                else:
+                    q.tensor_copy(T.yt[:, cols(m)], bank("v" + t)).then_inc(S[op], 1)
+
+    run(g.sync, SYNC)
+    run(A, SCALAR)
+    run(V, VECTOR)
+    run(g, POOL)
+    run(P, TENSOR)
+    g.sync.wait_ge(S.yd, 16 * sum(op[0] == "Y" for op in SYNC + SCALAR))

@@ -9,16 +9,18 @@ N7 = K * (NR - 1)
 XP = {"0": (0, 128), "1": (128, 256)}
 WP = {"0": (0, 4), "1": (4, 8), "2": (8, 10), "2b": (10, 12), "3": (12, 14), "3b": (14, 16)}
 VP = {"0": (0, 1), "1": (1, 2), "2": (2, 3), "3": (3, 4)}
-SP = {"0": (0, 12), "1": (12, 24)}
+SP = {"0": (10, N7), "1": (0, 10)}
 NE = {"c": 2, "s": 2}
 LP = 32
-SYNC = "Ln0 Lx0 Lx1 Lw0 ?xl1 Lw1 Lw2 ?locs Lw2b Lw3 Lw3b Lv0 Lv1 Lv2 Lv3 Y0 Y1 Y2 Y3".split()
-POOL = "Rs Rc ?locs ?locc".split()
-VECTOR = ("Z C x0 x1 S1 P0 P1 Co D O w0 w1 w2 "
-          "p0 p1 p23 w2b e03 w3 e12 w3b h0 e21 u0 u1 h1 e30 u2 h2 e33 u3 h3 y3").split()
+TOKAT = (0, 2, 3, 4)
+HAT = (0, 2, 1, 3)
+SYNC = "Ln0 Lx0 Lx1 Lw0 ?xl1 Lw1 Lw2 Lw2b ?go Lw3 Lw3b Lv0 Lv1 Lv2 Lv3 Y0 Y1 Y2 Y3".split()
+POOL = "Rs01 Rc01 !go ?locs ?locc".split()
+VECTOR = ("z C x0 x1 S1 P0 P1 Co D Z O w0 w1 w2 w2b "
+          "p0 p1 p23 w3 e02 w3b e11 h0 u0 e20 u1 h1 u2 e30 e32 h2 u3 h3 y2 y3").split()
 TENSOR = "m00 m01 m02 m03 m10 m11 m12 m13 m20 m21 m22 m23 m30 m31 m32 m33 v0 v1 v2 v3".split()
 SCALAR = ("Ln1 Lo0 Lo1 S0 Q "
-          "s0 s1 s23 e00 e01 e02 e10 e11 e13 e20 e22 e23 e31 e32 y0 y1 y2").split()
+          "s0 s1 s23 e00 e01 e03 e10 e12 e13 e21 e22 e23 e31 e33 y0 y1").split()
 SCRATCH = {
     "snt": ("sbuf", [LP, 24], "int32"),
     "sot": ("sbuf", [LP, 32], "int32"),
@@ -32,8 +34,8 @@ SCRATCH = {
     "zt": ("sbuf", [128, 4 * EC], "bfloat16"),
     "landq": ("sbuf", [128, WIN], F8),
     "lands": ("sbuf", [128, WIN], "uint8"),
-    "tokq": ("sbuf", [128, E * EC], F8),
-    "toks": ("sbuf", [128, E * EC], "uint8"),
+    "tokq": ("sbuf", [128, (E + 1) * EC], F8),
+    "toks": ("sbuf", [128, (E + 1) * EC], "uint8"),
     "wt": ("sbuf", [128, 2048 * E], "bfloat16"),
     "wq": ("sbuf", [128, 512 * E], F8),
     "ws": ("sbuf", [128, 512 * E], "uint8"),
@@ -48,7 +50,7 @@ SCRATCH = {
 for _i in range(8):
     SCRATCH["ps%d" % _i] = ("psum", [128, 512], "float32")
 PICKS = {_k + _d: _o for _o in VECTOR + SCALAR if _o[0] in "ps" for _k in _o[0] for _d in _o[1:]}
-SEMAPHORES = ["snl", "sol", "zm", "arrc", "arrs", "locc", "locs", "yd"]
+SEMAPHORES = ["snl", "sol", "zm", "arrc", "arrs", "locc", "locs", "yd", "go"]
 SEMAPHORES += ["xl" + _t for _t in XP] + ["wl" + _t for _t in WP] + ["vl" + _t for _t in VP]
 SEMAPHORES += sorted({_o for _o in TENSOR + VECTOR + SCALAR if _o[0] in "ZCDxwuPSOQpsmehvy"})
 
@@ -60,17 +62,18 @@ def rank_program(g, core, T, topo):
     S, V, A, P = T.sem, g.vector, g.scalar, g.tensor
     COPY, RELU = ActivationFunctionType.Copy, ActivationFunctionType.Relu
     narr = 2 * (NR - 1)
-    o0 = K * NR
+    o0 = N7 + N7 % 2
     own = EC + CAPP * r
-    full = {"snl": LP, "sol": LP, "C": 128 // LP, "D": 128 // LP, }
+    runs = [x for x in ((0, 0, K * r), (K * r, K * (r + 1), K * (NR - 1 - r)), (o0, K * r, K)) if x[2]]
+    full = {"snl": LP, "sol": LP, "C": (len(runs) - 1) * 128 // LP, "Co": 128 // LP, "D": 128 // LP}
     for k in NE:
         full["arr" + k] = full["loc" + k] = NE[k] * (NR - 1)
 
     def u32(ap):
         return ap.bitcast(dt.uint32)
 
-    def bank(op):
-        return T["ps%d" % (TENSOR.index(op) % 8)][:, 0:EC]
+    def bank(op, n=1):
+        return T["ps%d" % (TENSOR.index(op) % 8)][:, 0:EC * n]
 
     def freed(op):
         i = TENSOR.index(op) - 8
@@ -94,11 +97,13 @@ def rank_program(g, core, T, topo):
             use = e[1::2][2 * near:2 * near + 2]
             near += 1
         rid, pid, _ = topo.addr(dst)
-        plan.append((d, DstId(rid=rid, pnc=pid), use))
+        plan.append((d if d < r else d - 1, DstId(rid=rid, pnc=pid), use))
 
-    def send(codes):
+    def send(codes, parts):
         ts = []
         for j, did, use in plan:
+            if not any(SP[u][0] <= K * j < SP[u][1] for u in parts):
+                continue
             mask = sum(1 << k for k in use[:NE["c" if codes else "s"]])
             if codes:
                 src = T.slotq[:, CAPP * j:CAPP * j + CAPP].bitcast(dt.uint8)
@@ -143,27 +148,27 @@ def rank_program(g, core, T, topo):
             k, t = op[0], op[1:]
             if k == "?":
                 need(t)
+            elif k == "!":
+                q.sem_inc(S[t], 1)
             elif k == "L":
                 load(q, t)
             elif k == "R":
-                need(*[("P" if t == "c" else "S") + u for u in SP])
-                send(t == "c")
+                need(*[("P" if t[0] == "c" else "S") + u for u in t[1:]])
+                send(t[0] == "c", t[1:])
             elif k == "Y":
                 need(*["y" + u for u in t])
                 c = cols(int(t[0]), len(t))
                 q.dma_start(T.y[:, c], T.yt[:, c]).then_inc(S.yd, 16)
-            elif k == "Z":
+            elif k == "z":
                 q.memset(T.zt[:, :], 0.0).then_inc(S.zm, 1)
+            elif k == "Z":
                 need("zm")
                 q.quantize_mx(T.landq[:, 0:EC], T.lands[:, 0:EC], T.zt[:, :]).then_inc(S.Z, 1)
             elif k == "C":
-                if t:
-                    need("C")
-                    q.tensor_copy(T.offs[:, o0:o0 + K], T.offs[:, K * r:K * r + K]).then_inc(S[op], 1)
-                else:
-                    need("snl")
+                need("snl")
+                for to, a, n in (runs[-1:] if t else runs[:-1]):
                     for p in range(0, 128, LP):
-                        q.tensor_copy(T.offs[p:p + LP, 0:o0], T.snt[:, :]).then_inc(S[op], 1)
+                        q.tensor_copy(T.offs[p:p + LP, to:to + n], T.snt[:, a:a + n]).then_inc(S[op], 1)
             elif k == "D":
                 need("sol")
                 for p in range(0, 128, LP):
@@ -190,25 +195,33 @@ def rank_program(g, core, T, topo):
             elif k in "ps":
                 m, n, codes = int(t[0]), len(t), k == "p"
                 need("D", "Z", *(("O", "arrc") if codes else ("Q", "arrs")))
-                pick(q, codes, (T.tokq if codes else T.toks)[:, cols(m, n)], (T.landq if codes else T.lands)[:, :],
+                pick(q, codes, (T.tokq if codes else T.toks)[:, cols(TOKAT[m], n)], (T.landq if codes else T.lands)[:, :],
                      T.offt[:, 8 * m:8 * (m + n)], S[op])
             elif k == "m":
-                m, b = int(t[0]), int(t[1])
-                need(PICKS["s%d" % m], "w" + piece(WP, 4 * m + b), PICKS["p%d" % m], *freed(op))
-                c = 512 * m + 128 * b
-                q.matmul_mx(bank(op), T.wq[:, c:c + 128], T.ws[:, c:c + 128], T.tokq[:, cols(m)], T.toks[:, cols(m)], True, True).then_inc(S[op], 1)
+                ms, b = [int(u) for u in t[:-1]], int(t[-1])
+                for m in ms:
+                    need(PICKS["s%d" % m], "w" + piece(WP, 4 * m + b), PICKS["p%d" % m])
+                need(*freed(op))
+                for m in ms:
+                    n = 2 if m != ms[-1] else 1
+                    c, to = 512 * m + 128 * b, cols(TOKAT[m] + 1 - n, n)
+                    if n == 2:
+                        need("Z")
+                    mm = q.matmul_mx(bank(op, n), T.wq[:, c:c + 128], T.ws[:, c:c + 128], T.tokq[:, to], T.toks[:, to], m == ms[0], m == ms[-1])
+                mm.then_inc(S[op], 1)
             elif k == "e":
-                m, b = int(t[0]), int(t[1])
+                n, b = len(t) - 1, int(t[-1])
                 need("m" + t)
-                h = T.ht[:, 512 * m + b:512 * m + 512:4]
+                c = 512 * HAT[int(t[-2])]
+                h = T.ht[:, c + b:c + 512 * n:4]
                 if q is A:
-                    q.activation(h, bank("m" + t), RELU, scale=0.05).then_inc(S[op], 1)
+                    q.activation(h, bank("m" + t, n), RELU, scale=0.05).then_inc(S[op], 1)
                 else:
-                    q.tensor_scalar(h, bank("m" + t), 0.0, 0.05, AluOpType.max, AluOpType.mult).then_inc(S[op], 1)
+                    q.tensor_scalar(h, bank("m" + t, n), 0.0, 0.05, AluOpType.max, AluOpType.mult).then_inc(S[op], 1)
             elif k == "h":
                 m = int(t)
-                need(*["e%d%d" % (m, c) for c in range(4)])
-                q.quantize_mx(T.hq[:, cols(m)], T.hs[:, cols(m)], T.ht[:, 512 * m:512 * m + 512]).then_inc(S[op], 1)
+                need(*[u for u in VECTOR + SCALAR if u[0] == "e" and t in u[1:-1]])
+                q.quantize_mx(T.hq[:, cols(m)], T.hs[:, cols(m)], T.ht[:, 512 * HAT[m]:512 * HAT[m] + 512]).then_inc(S[op], 1)
             elif k == "v":
                 m = int(t)
                 need("u" + piece(VP, m), "h" + t, *freed(op))

from concourse.bass import DstId, RemoteDMATransfer
from concourse.mybir import dt, AluOpType, ActivationFunctionType

E, EC, CAPP, NR, TOK = 4, 128, 48, 8, 256
F8 = "float8_e4m3fn_x4"
WIN = EC + NR * CAPP
K = CAPP // 16
N7 = K * (NR - 1)
XP = {"0": (0, 128), "1": (128, 256)}
WP = {"0": (0, 4), "1": (4, 8), "2": (8, 10), "2b": (10, 12), "3": (12, 14), "3b": (14, 16)}
VP = {"0": (0, 1), "1": (1, 2), "2": (2, 3), "3": (3, 4)}
SP = {"0": (10, N7), "1": (0, 10)}
NE = {"c": 2, "s": 2}
LP = 32
TOKAT = (0, 2, 3, 4)
HAT = (0, 2, 1, 3)
SYNC = "Ln0 Lx0 Lx1 Lw0 ?xl1 Lw1 Lw2 Lw2b ?go Lw3 Lw3b Lv0 Lv1 Lv2 Lv3 Y0 Y1 Y2 Y3".split()
POOL = "Rs01 Rc01 !go ?locs ?locc".split()
VECTOR = ("z C x0 x1 S1 P0 P1 Co D Z O w0 w1 w2 w2b "
          "p0 p1 p23 w3 e02 w3b e11 h0 u0 e20 u1 h1 u2 e30 e32 h2 u3 h3 y2 y3").split()
TENSOR = "m00 m01 m02 m03 m10 m11 m12 m13 m20 m21 m22 m23 m30 m31 m32 m33 v0 v1 v2 v3".split()
SCALAR = ("Ln1 Lo0 Lo1 S0 Q "
          "s0 s1 s23 e00 e01 e03 e10 e12 e13 e21 e22 e23 e31 e33 y0 y1").split()
SCRATCH = {
    "snt": ("sbuf", [LP, 24], "int32"),
    "sot": ("sbuf", [LP, 32], "int32"),
    "offs": ("sbuf", [128, 32], "uint16"),
    "offt": ("sbuf", [128, 32], "uint16"),
    "xt": ("sbuf", [128, 4 * TOK], "bfloat16"),
    "xq": ("sbuf", [128, TOK], F8),
    "xs": ("sbuf", [128, TOK], "uint8"),
    "slotq": ("sbuf", [128, NR * CAPP], F8),
    "slots": ("sbuf", [128, NR * CAPP], "uint8"),
    "zt": ("sbuf", [128, 4 * EC], "bfloat16"),
    "landq": ("sbuf", [128, WIN], F8),
    "lands": ("sbuf", [128, WIN], "uint8"),
    "tokq": ("sbuf", [128, (E + 1) * EC], F8),
    "toks": ("sbuf", [128, (E + 1) * EC], "uint8"),
    "wt": ("sbuf", [128, 2048 * E], "bfloat16"),
    "wq": ("sbuf", [128, 512 * E], F8),
    "ws": ("sbuf", [128, 512 * E], "uint8"),
    "vt": ("sbuf", [128, 512 * E], "bfloat16"),
    "vq": ("sbuf", [128, 128 * E], F8),
    "vs": ("sbuf", [128, 128 * E], "uint8"),
    "ht": ("sbuf", [128, 4 * EC * E], "bfloat16"),
    "hq": ("sbuf", [128, EC * E], F8),
    "hs": ("sbuf", [128, EC * E], "uint8"),
    "yt": ("sbuf", [128, EC * E], "float32"),
}
for _i in range(8):
    SCRATCH["ps%d" % _i] = ("psum", [128, 512], "float32")
PICKS = {_k + _d: _o for _o in VECTOR + SCALAR if _o[0] in "ps" for _k in _o[0] for _d in _o[1:]}
SEMAPHORES = ["snl", "sol", "zm", "arrc", "arrs", "locc", "locs", "yd", "go"]
SEMAPHORES += ["xl" + _t for _t in XP] + ["wl" + _t for _t in WP] + ["vl" + _t for _t in VP]
SEMAPHORES += sorted({_o for _o in TENSOR + VECTOR + SCALAR if _o[0] in "ZCDxwuPSOQpsmehvy"})


def rank_program(g, core, T, topo):
    r = T.rank_of(core)
    if r is None:
        return
    S, V, A, P = T.sem, g.vector, g.scalar, g.tensor
    COPY, RELU = ActivationFunctionType.Copy, ActivationFunctionType.Relu
    narr = 2 * (NR - 1)
    o0 = N7 + N7 % 2
    own = EC + CAPP * r
    runs = [x for x in ((0, 0, K * r), (K * r, K * (r + 1), K * (NR - 1 - r)), (o0, K * r, K)) if x[2]]
    full = {"snl": LP, "sol": LP, "C": (len(runs) - 1) * 128 // LP, "Co": 128 // LP, "D": 128 // LP}
    for k in NE:
        full["arr" + k] = full["loc" + k] = NE[k] * (NR - 1)

    def u32(ap):
        return ap.bitcast(dt.uint32)

    def bank(op, n=1):
        return T["ps%d" % (TENSOR.index(op) % 8)][:, 0:EC * n]

    def freed(op):
        i = TENSOR.index(op) - 8
        return [{"m": "e", "v": "y"}[TENSOR[i][0]] + TENSOR[i][1:]] if i >= 0 else []

    def cols(m, n=1):
        return slice(EC * m, EC * (m + n))

    def piece(pieces, i):
        return [t for t in pieces if pieces[t][0] <= i < pieces[t][1]][0]

    far, near, plan = 0, 0, []
    for i in range(1, NR):
        d = (r + i) % NR
        dst = T.cores[d]
        e = topo.engines(core, dst)
        if topo.die(dst) != topo.die(core):
            use = e[0::2][2 * far:2 * far + 2]
            far += 1
        else:
            use = e[1::2][2 * near:2 * near + 2]
            near += 1
        rid, pid, _ = topo.addr(dst)
        plan.append((d if d < r else d - 1, DstId(rid=rid, pnc=pid), use))

    def send(codes, parts):
        ts = []
        for j, did, use in plan:
            if not any(SP[u][0] <= K * j < SP[u][1] for u in parts):
                continue
            mask = sum(1 << k for k in use[:NE["c" if codes else "s"]])
            if codes:
                src = T.slotq[:, CAPP * j:CAPP * j + CAPP].bitcast(dt.uint8)
                dst = T.landq[:, own:own + CAPP].bitcast(dt.uint8)
            else:
                src = T.slots[:, CAPP * j:CAPP * j + CAPP]
                dst = T.lands[:, own:own + CAPP]
            ts.append(RemoteDMATransfer(dst_ids=[did], dma_engine_mask=mask, remote_sem=S.arrc if codes else S.arrs, src=src, dst=dst))
        g.remote_dma_fused(ts, local_sem=S.locc if codes else S.locs)

    def load(q, op):
        k, t = op[0], op[1:]
        if k == "x":
            a, b = XP[t]
            q.dma_start(T.xt[:, 4 * a:4 * b], T.x[:, 4 * a:4 * b]).then_inc(S["xl" + t], 16)
        elif k in "no":
            i = int(t)
            dst, src = (T.snt, T.sn) if k == "n" else (T.sot, T.so)
            q.dma_start(dst[16 * i:16 * i + 16, :], src[:, :]).then_inc(S.snl if k == "n" else S.sol, 16)
        else:
            a, b = (WP if k == "w" else VP)[t]
            q.dma_start(T[k + "t"][:, 512 * a:512 * b], T[k][:, 512 * a:512 * b]).then_inc(S[k + "l" + t], 16)

    def pick(q, codes, to, win, off, done):
        if codes:
            q.tensor_copy(u32(to), u32(win).indirect(off)).then_inc(done, 1)
        elif q is A:
            q.activation(to, win.indirect(off), COPY).then_inc(done, 1)
        else:
            q.tensor_copy(to, win.indirect(off)).then_inc(done, 1)

    def run(q, ops):
        seen = set()

        def need(*names):
            for s in names:
                if s not in seen:
                    seen.add(s)
                    q.wait_ge(S[s], full.get(s, 16 if s[1:2] == "l" else 1))

        for op in ops:
            k, t = op[0], op[1:]
            if k == "?":
                need(t)
            elif k == "!":
                q.sem_inc(S[t], 1)
            elif k == "L":
                load(q, t)
            elif k == "R":
                need(*[("P" if t[0] == "c" else "S") + u for u in t[1:]])
                send(t[0] == "c", t[1:])
            elif k == "Y":
                need(*["y" + u for u in t])
                c = cols(int(t[0]), len(t))
                q.dma_start(T.y[:, c], T.yt[:, c]).then_inc(S.yd, 16)
            elif k == "z":
                q.memset(T.zt[:, :], 0.0).then_inc(S.zm, 1)
            elif k == "Z":
                need("zm")
                q.quantize_mx(T.landq[:, 0:EC], T.lands[:, 0:EC], T.zt[:, :]).then_inc(S.Z, 1)
            elif k == "C":
                need("snl")
                for to, a, n in (runs[-1:] if t else runs[:-1]):
                    for p in range(0, 128, LP):
                        q.tensor_copy(T.offs[p:p + LP, to:to + n], T.snt[:, a:a + n]).then_inc(S[op], 1)
            elif k == "D":
                need("sol")
                for p in range(0, 128, LP):
                    q.tensor_scalar(T.offt[p:p + LP, :], T.sot[:, :], EC, None, AluOpType.add).then_inc(S.D, 1)
            elif k == "x":
                a, b = XP[t]
                need("xl" + t)
                q.quantize_mx(T.xq[:, a:b], T.xs[:, a:b], T.xt[:, 4 * a:4 * b]).then_inc(S[op], 1)
            elif k in "wu":
                n = "w" if k == "w" else "v"
                a, b = (WP if k == "w" else VP)[t]
                need(n + "l" + t)
                q.quantize_mx(T[n + "q"][:, 128 * a:128 * b], T[n + "s"][:, 128 * a:128 * b], T[n + "t"][:, 512 * a:512 * b]).then_inc(S[op], 1)
            elif k in "PSOQ":
                need("C" if k in "PS" else "Co", *["x" + u for u in XP])
                codes = k in "PO"
                if k in "PS":
                    a, b = SP[t]
                    to = (T.slotq if codes else T.slots)[:, 16 * a:16 * b]
                else:
                    a, b = o0, o0 + K
                    to = (T.landq if codes else T.lands)[:, own:own + CAPP]
                pick(q, codes, to, (T.xq if codes else T.xs)[:, :], T.offs[:, a:b], S[op])
            elif k in "ps":
                m, n, codes = int(t[0]), len(t), k == "p"
                need("D", "Z", *(("O", "arrc") if codes else ("Q", "arrs")))
                pick(q, codes, (T.tokq if codes else T.toks)[:, cols(TOKAT[m], n)], (T.landq if codes else T.lands)[:, :],
                     T.offt[:, 8 * m:8 * (m + n)], S[op])
            elif k == "m":
                ms, b = [int(u) for u in t[:-1]], int(t[-1])
                for m in ms:
                    need(PICKS["s%d" % m], "w" + piece(WP, 4 * m + b), PICKS["p%d" % m])
                need(*freed(op))
                for m in ms:
                    n = 2 if m != ms[-1] else 1
                    c, to = 512 * m + 128 * b, cols(TOKAT[m] + 1 - n, n)
                    if n == 2:
                        need("Z")
                    mm = q.matmul_mx(bank(op, n), T.wq[:, c:c + 128], T.ws[:, c:c + 128], T.tokq[:, to], T.toks[:, to], m == ms[0], m == ms[-1])
                mm.then_inc(S[op], 1)
            elif k == "e":
                n, b = len(t) - 1, int(t[-1])
                need("m" + t)
                c = 512 * HAT[int(t[-2])]
                h = T.ht[:, c + b:c + 512 * n:4]
                if q is A:
                    q.activation(h, bank("m" + t, n), RELU, scale=0.05).then_inc(S[op], 1)
                else:
                    q.tensor_scalar(h, bank("m" + t, n), 0.0, 0.05, AluOpType.max, AluOpType.mult).then_inc(S[op], 1)
            elif k == "h":
                m = int(t)
                need(*[u for u in VECTOR + SCALAR if u[0] == "e" and t in u[1:-1]])
                q.quantize_mx(T.hq[:, cols(m)], T.hs[:, cols(m)], T.ht[:, 512 * HAT[m]:512 * HAT[m] + 512]).then_inc(S[op], 1)
            elif k == "v":
                m = int(t)
                need("u" + piece(VP, m), "h" + t, *freed(op))
                q.matmul_mx(bank(op), T.vq[:, cols(m)], T.vs[:, cols(m)], T.hq[:, cols(m)], T.hs[:, cols(m)], True, True).then_inc(S[op], 1)
            elif k == "y":
                m = int(t)
                need("v" + t)
                if q is A:
                    q.activation(T.yt[:, cols(m)], bank("v" + t), COPY).then_inc(S[op], 1)
                else:
                    q.tensor_copy(T.yt[:, cols(m)], bank("v" + t)).then_inc(S[op], 1)

    run(g.sync, SYNC)
    run(A, SCALAR)
    run(V, VECTOR)
    run(g, POOL)
    run(P, TENSOR)
    g.sync.wait_ge(S.yd, 16 * sum(op[0] == "Y" for op in SYNC + SCALAR))
